import numpy as np
import ml_dtypes


def mxq(x, axis, fmt="e4m3"):
    dtype, down = {"e4m3": (ml_dtypes.float8_e4m3fn, 7), "e5m2": (ml_dtypes.float8_e5m2, 14)}[fmt]
    v = np.moveaxis(np.asarray(x, np.float32).astype(ml_dtypes.bfloat16).astype(np.float64), axis, -1)
    blocks = v.reshape(v.shape[:-1] + (-1, 32))
    amax = np.abs(blocks).max(-1, keepdims=True)
    byte = np.maximum(np.where(amax > 0, np.frexp(amax)[1] - 1 + 127, 0) - down, 1)
    scale = np.exp2(byte - 127.0)
    codes = (blocks / scale).astype(np.float32).astype(dtype).astype(np.float64)
    return np.moveaxis((codes * scale).reshape(v.shape), -1, axis)


WIDE = False


def mx_kscale(k):
    if not WIDE:
        return np.ones(k)
    levels = np.array([10, -10, 5, -5, 0])
    if k % 512:
        return np.exp2(np.random.permutation(np.resize(levels, k // 32))).repeat(32)
    a = np.empty((k // 512, 16))
    for p in range(k // 512):
        a[p, :8] = np.random.permutation(np.resize(levels, 8))
        for g in range(8):
            far = levels[np.abs(levels - a[p, g]) >= 10]
            a[p, g + 8] = far[np.random.randint(len(far))]
    return np.exp2(a.ravel()).repeat(32)


def f64(x):
    return np.asarray(x).astype(np.float64)


def striped(idx):
    return np.tile(idx.reshape(-1, 16).T, (8, 1)).astype(np.uint16)


def unstriped(offs):
    return offs[:16].T.reshape(-1).astype(np.int64)


def pack_weight(w):
    k, n = w.shape
    w = f64(np.asarray(w, np.float32).astype(ml_dtypes.bfloat16)).reshape(k // 32, 32, n)
    amax = np.abs(w).max(1)
    byte = np.clip(np.where(amax > 0, np.frexp(amax)[1] - 1 + 127 - 7, 1), 1, 254)
    scaled = (w * np.exp2(127.0 - byte)[:, None, :]).reshape(k, n).astype(np.float32)
    words = np.ascontiguousarray(scaled.reshape(k // 512, 128, 4, n).transpose(0, 1, 3, 2)).astype(ml_dtypes.float8_e4m3fn).view(np.uint8)
    return words, np.ascontiguousarray(byte.astype(np.uint8).reshape(k // 512, 16, n))


def unpack_weight(words, scales):
    g, p, n, _ = words.shape
    vals = np.ascontiguousarray(words).view(ml_dtypes.float8_e4m3fn).astype(np.float64) * np.repeat(np.exp2(scales.astype(np.float64) - 127.0), 8, axis=1)[..., None]
    return vals.transpose(0, 1, 3, 2).reshape(g * 512, n)


K, T, S, N, U, D = 512, 1024, 512, 256, 256, 2
P = 2 ** 7


def setup_inputs():
    n = np.random.standard_normal
    s = mx_kscale(K)[:, None]
    packed_xT = pack_weight(n((K, T)) * s)
    return {
        "x_words": packed_xT[0],
        "x_scales": packed_xT[1],
        "w1": (n((K, N)) / np.sqrt(K) / s).astype(np.float32),
        "w2": (n((K, N)) / np.sqrt(K) / s).astype(np.float32),
        "w3": (n((K, N)) / np.sqrt(K) / s).astype(np.float32),
        "px": (n((N, U))).astype(np.float32),
        "py": (n((N, U))).astype(np.float32),
        "wgt": (np.tile(np.random.uniform(0.1, 0.6, (D, 1, U)), (1, P, 1))).astype(np.float32),
        "offs": striped(np.random.permutation(T)[:S]),
        "jt1": striped(np.random.randint(0, S, U)),
        "jt2": striped(np.random.randint(0, S, U)),
    }


def reference(x_words, x_scales, w1, w2, w3, px, py, wgt, offs, jt1, jt2):
    xq = unpack_weight(x_words, x_scales)[:, unstriped(offs)]
    ra = mxq(f64(w1), 0, "e4m3").T @ xq
    aa = f64(wgt)[0, :1] * ra[:, unstriped(jt1)] + f64(wgt)[1, :1] * ra[:, unstriped(jt2)]
    rb = mxq(f64(w2), 0, "e4m3").T @ xq
    bb = f64(wgt)[0, :1] * rb[:, unstriped(jt1)] + f64(wgt)[1, :1] * rb[:, unstriped(jt2)]
    tr = mxq(f64(w3), 0, "e4m3").T @ xq
    return (aa * f64(px) - (bb * f64(py))) / (np.sqrt((aa) ** 2 + (bb) ** 2 + 0.1)) + f64(wgt)[0, :1] * tr[:, unstriped(jt1)] + f64(wgt)[1, :1] * tr[:, unstriped(jt2)]

@@ -1,0 +1,161 @@
+from contextlib import ExitStack
+
+import concourse.mybir as mybir
+from concourse.masks import make_identity
+
+K, T, S, N, U = 512, 1024, 512, 256, 256
+FLOPS = 3 * 2 * K * N * S
+
+F32 = mybir.dt.float32
+BF16 = mybir.dt.bfloat16
+I32 = mybir.dt.int32
+U32 = mybir.dt.uint32
+U16 = mybir.dt.uint16
+U8 = mybir.dt.uint8
+FP8X4 = mybir.dt.float8_e4m3fn_x4
+ACT = mybir.ActivationFunctionType
+MULT = mybir.AluOpType.mult
+ADD = mybir.AluOpType.add
+
+P = 128
+PACK = 4
+BLOCKS = N // P
+CHUNKS = U // P
+EPS = 0.1
+
+
+def tile_picked_yskinlb_norm_p_kernel(
+    tc, x_words, x_scales, w1, w2, w3, px, py, wgt, offs, jt1, jt2, out
+):
+    nc = tc.nc
+    with ExitStack() as ctx:
+        keep = ctx.enter_context(tc.tile_pool(name="keep", bufs=1))
+        psum = ctx.enter_context(tc.psum_pool(name="psum", bufs=1))
+
+        def bank(i, shape):
+            return psum.tile(shape, F32, name="bank%d" % i)
+
+        def sb(name, shape, dtype):
+            return keep.tile(shape, dtype, name=name, align_bytes=64)
+
+        offs_sb = keep.tile([P, S // 16], U16, name="offs_sb")
+        jt_sb = [keep.tile([P, U // 16], U16, name="jt%d_sb" % d) for d in range(2)]
+        words = sb("words", [P, T], I32)
+        scales = sb("scales", [P, T], U8)
+        w_raw = [sb("w_raw%d" % q, [P, PACK, N], F32) for q in range(3)]
+        wgt_sb = sb("wgt_sb", [P, 2, U], F32)
+        px_sb = sb("px_sb", [P, BLOCKS, U], F32)
+        py_sb = sb("py_sb", [P, BLOCKS, U], F32)
+        ident = sb("ident", [P, P], F32)
+        one = sb("one", [P, 1], F32)
+        warm = sb("warm", [P, 1], F32)
+
+        nc.gpsimd.memset(scales[:].bitcast(I32), 0)
+        nc.gpsimd.memset(one[:], 1.0)
+        make_identity(nc, ident[:])
+
+        nc.sync.dma_start(offs_sb[:], offs)
+        for q in range(4):
+            nc.scalar.dma_start(scales[32 * q : 32 * q + 4, :].bitcast(I32), x_scales[0, 4 * q : 4 * q + 4, :].bitcast(I32))
+        nc.sync.dma_start(w_raw[0][:], w1.rearrange("(p j) m -> p j m", j=PACK))
+        nc.sync.dma_start(words[:], x_words[0].rearrange("p n t -> p (n t)").bitcast(I32))
+        nc.sync.dma_start(w_raw[1][:], w2.rearrange("(p j) m -> p j m", j=PACK))
+        nc.sync.dma_start(jt_sb[0][:], jt1)
+        nc.sync.dma_start(jt_sb[1][:], jt2)
+        nc.sync.dma_start(wgt_sb[:], wgt.rearrange("d p r -> p d r"))
+        nc.sync.dma_start(w_raw[2][:], w3.rearrange("(p j) m -> p j m", j=PACK))
+        nc.sync.dma_start(px_sb[:], px.rearrange("(b p) r -> p b r", p=P))
+        nc.sync.dma_start(py_sb[:], py.rearrange("(b p) r -> p b r", p=P))
+
+        nc.scalar.activation(warm[:], one[:], ACT.Abs_reciprocal_sqrt)
+
+        picked_words = sb("picked_words", [P, S], U32)
+        picked_scales = sb("picked_scales", [P, S], U8)
+        nc.vector.tensor_copy(picked_scales[:], scales[:].indirect(offs_sb[:]))
+        for h in range(2):
+            nc.vector.tensor_copy(picked_words[:, h * 256 : (h + 1) * 256], words[:].bitcast(U32).indirect(offs_sb[:, h * 16 : (h + 1) * 16]))
+
+        def product(q, b, cast, bank_nos):
+            grouped = sb("grouped%d%d" % (q, b), [P, P, PACK], BF16)
+            cast(grouped[:], w_raw[q][:, :, b * P : (b + 1) * P].rearrange("p j m -> p m j"))
+            codes = sb("codes%d%d" % (q, b), [P, P], U32)
+            plane = sb("plane%d%d" % (q, b), [P, P], U8)
+            nc.vector.quantize_mx(codes[:].bitcast(FP8X4), plane[:], grouped[:].rearrange("p m j -> p (m j)"))
+            rows = sb("rows%d%d" % (q, b), [P, S], F32)
+            width = S // len(bank_nos)
+            for h, bank_no in enumerate(bank_nos):
+                cols = slice(h * width, (h + 1) * width)
+                acc = bank(bank_no, [P, width])
+                nc.tensor.matmul_mx(
+                    acc[:], lhsT=codes[:].bitcast(FP8X4), lhsT_scale=plane[:],
+                    rhs=picked_words[:, cols].bitcast(FP8X4), rhs_scale=picked_scales[:, cols], start=True, stop=True,
+                )
+                nc.scalar.copy(rows[:, cols], acc[:])
+            return rows
+
+        def fetch(dst, rows, d):
+            nc.vector.tensor_tensor(dst.rearrange("p c r -> p (c r)"), rows[:].indirect(jt_sb[d][:]), wgt_sb[:, d, :], MULT)
+
+        def turn(dst, src, first, last):
+            for c in range(CHUNKS):
+                nc.tensor.matmul(dst[:, c, :], src[:, c, :], ident[:], start=(first and c == 0), stop=(last and c == CHUNKS - 1), is_transpose=True)
+
+        def turn_rest(name, src, sign, bank_no):
+            both = bank(bank_no, [P, BLOCKS, CHUNKS, P])
+            for b in range(BLOCKS):
+                turn(both[:, b], src[:, b, :].rearrange("p (c r) -> p c r", c=CHUNKS), b == 0, b == BLOCKS - 1)
+            turned = sb(name, [P, BLOCKS, CHUNKS, P], F32)
+            nc.scalar.activation(turned[:], both[:], ACT.Copy, scale=sign)
+            return turned
+
+        def mix(q, b, rows, bank_no):
+            mixed = bank(bank_no, [P, CHUNKS, P])
+            for d in range(2):
+                term = sb("term%d%d%d" % (q, b, d), [P, CHUNKS, P], F32)
+                fetch(term[:], rows, d)
+                turn(mixed, term, d == 0, d == 1)
+            return mixed
+
+        def spread(q, b, mixed, rest_t, sumsq, numer):
+            square = sb("square%d%d" % (q, b), [P, CHUNKS, P], F32)
+            nc.scalar.activation(square[:], mixed[:], ACT.Square)
+            moved = sb("moved%d%d" % (q, b), [P, CHUNKS, P], F32)
+            nc.vector.tensor_tensor(moved[:], mixed[:], rest_t[:, b], MULT)
+            turn(sumsq, square, q == 0, q == 1)
+            turn(numer, moved, q == 0, q == 1)
+
+        def normalise(b, sumsq, numer):
+            inv = sb("inv%d" % b, [P, CHUNKS, P], F32)
+            nc.scalar.activation(inv[:], sumsq[:], ACT.Abs_reciprocal_sqrt, bias=EPS)
+            rotated = sb("rotated%d" % b, [P, CHUNKS, P], F32)
+            nc.vector.tensor_tensor(rotated[:], numer[:], inv[:], MULT)
+            return rotated
+
+        def finish(b, rotated, terms):
+            half = sb("half%d" % b, [P, CHUNKS, P], F32)
+            nc.vector.tensor_tensor(half[:], rotated[:], terms[0], ADD)
+            result = sb("result%d" % b, [P, CHUNKS, P], F32)
+            nc.vector.tensor_tensor(result[:], half[:], terms[1], ADD)
+            nc.sync.dma_start(out[b * P : (b + 1) * P, :], result[:].rearrange("p c r -> p (c r)"))
+
+        ra = [product(0, 0, nc.scalar.copy, [6, 0]), product(0, 1, nc.vector.tensor_copy, [1])]
+        rb = [product(1, 0, nc.vector.tensor_copy, [2]), product(1, 1, nc.scalar.copy, [3])]
+        tr = [product(2, b, nc.scalar.copy, [b]) for b in range(BLOCKS)]
+        aa = [mix(0, b, ra[b], 2 + b) for b in range(BLOCKS)]
+        px_t = turn_rest("px_t", px_sb, 1.0, 4)
+        py_t = turn_rest("py_t", py_sb, -1.0, 5)
+        sumsq = [bank(4, [P, CHUNKS, P]), bank(6, [P, CHUNKS, P])]
+        numer = [bank(5, [P, CHUNKS, P]), bank(7, [P, CHUNKS, P])]
+        bb0 = mix(1, 0, rb[0], 0)
+        for b in range(BLOCKS):
+            spread(0, b, aa[b], px_t, sumsq[b], numer[b])
+        bb = [bb0, mix(1, 1, rb[1], 1)]
+        shifts = []
+        for b in range(BLOCKS):
+            spread(1, b, bb[b], py_t, sumsq[b], numer[b])
+            second = sb("shift%d" % b, [P, CHUNKS, P], F32)
+            fetch(py_t[:, b], tr[b], 0)
+            fetch(second[:], tr[b], 1)
+            shifts.append([py_t[:, b], second[:]])
+        for b in range(BLOCKS):
+            finish(b, normalise(b, sumsq[b], numer[b]), shifts[b])

@@ -35,14 +35,16 @@ def tile_picked_yskinlb_norm_p_kernel(
         def bank(i, shape):
             return psum.tile(shape, F32, name="bank%d" % i)
 
-        def sb(name, shape, dtype):
-            return keep.tile(shape, dtype, name=name, align_bytes=64)
+        def sb(name, shape, dtype, tag=None):
+            return keep.tile(shape, dtype, name=name, tag=tag or name, align_bytes=64)
 
         offs_sb = keep.tile([P, S // 16], U16, name="offs_sb")
         jt_sb = [keep.tile([P, U // 16], U16, name="jt%d_sb" % d) for d in range(2)]
         words = sb("words", [P, T], I32)
         scales = sb("scales", [P, T], U8)
-        w_raw = [sb("w_raw%d" % q, [P, PACK, N], F32) for q in range(3)]
+        w1_raw = sb("w1_raw", [P, PACK, N], F32)
+        w2_raw = sb("w2_raw", [P, PACK, N], F32)
+        w3_raw = sb("w3_raw", [P, PACK, N], F32)
         wgt_sb = sb("wgt_sb", [P, 2, U], F32)
         px_sb = sb("px_sb", [P, BLOCKS, U], F32)
         py_sb = sb("py_sb", [P, BLOCKS, U], F32)
@@ -55,39 +57,43 @@ def tile_picked_yskinlb_norm_p_kernel(
         make_identity(nc, ident[:])
 
         nc.sync.dma_start(offs_sb[:], offs)
-        for q in range(4):
-            nc.scalar.dma_start(scales[32 * q : 32 * q + 4, :].bitcast(I32), x_scales[0, 4 * q : 4 * q + 4, :].bitcast(I32))
-        nc.sync.dma_start(w_raw[0][:], w1.rearrange("(p j) m -> p j m", j=PACK))
-        nc.sync.dma_start(words[:], x_words[0].rearrange("p n t -> p (n t)").bitcast(I32))
-        nc.sync.dma_start(w_raw[1][:], w2.rearrange("(p j) m -> p j m", j=PACK))
         nc.sync.dma_start(jt_sb[0][:], jt1)
         nc.sync.dma_start(jt_sb[1][:], jt2)
+        for q in range(4):
+            nc.sync.dma_start(scales[32 * q : 32 * q + 4, :].bitcast(I32), x_scales[0, 4 * q : 4 * q + 4, :].bitcast(I32))
+        nc.sync.dma_start(words[:], x_words[0].rearrange("p n t -> p (n t)").bitcast(I32))
+        nc.sync.dma_start(w1_raw[:], w1.rearrange("(p j) m -> p j m", j=PACK))
+        nc.sync.dma_start(w2_raw[:], w2.rearrange("(p j) m -> p j m", j=PACK))
         nc.sync.dma_start(wgt_sb[:], wgt.rearrange("d p r -> p d r"))
-        nc.sync.dma_start(w_raw[2][:], w3.rearrange("(p j) m -> p j m", j=PACK))
+        nc.sync.dma_start(w3_raw[:], w3.rearrange("(p j) m -> p j m", j=PACK))
         nc.sync.dma_start(px_sb[:], px.rearrange("(b p) r -> p b r", p=P))
         nc.sync.dma_start(py_sb[:], py.rearrange("(b p) r -> p b r", p=P))
 
         nc.scalar.activation(warm[:], one[:], ACT.Abs_reciprocal_sqrt)
 
-        picked_words = sb("picked_words", [P, S], U32)
         picked_scales = sb("picked_scales", [P, S], U8)
         nc.vector.tensor_copy(picked_scales[:], scales[:].indirect(offs_sb[:]))
-        for h in range(2):
-            nc.vector.tensor_copy(picked_words[:, h * 256 : (h + 1) * 256], words[:].bitcast(U32).indirect(offs_sb[:, h * 16 : (h + 1) * 16]))
+        picked_words = sb("picked_words", [P, S], U32)
+        nc.vector.tensor_copy(picked_words[:], words[:].bitcast(U32).indirect(offs_sb[:]))
 
-        def product(q, b, cast, bank_nos):
-            grouped = sb("grouped%d%d" % (q, b), [P, P, PACK], BF16)
-            cast(grouped[:], w_raw[q][:, :, b * P : (b + 1) * P].rearrange("p j m -> p m j"))
-            codes = sb("codes%d%d" % (q, b), [P, P], U32)
-            plane = sb("plane%d%d" % (q, b), [P, P], U8)
+        def quantise(name, raw, cast, stage):
+            width = raw.shape[2]
+            grouped = sb(name + "_grouped", [P, width, PACK], BF16, tag=stage)
+            cast(grouped[:].rearrange("p (c i) j -> p c j i", i=4), raw.rearrange("p j (c i) -> p c j i", i=4))
+            codes = sb(name + "_codes", [P, width], U32)
+            plane = sb(name + "_plane", [P, width], U8)
             nc.vector.quantize_mx(codes[:].bitcast(FP8X4), plane[:], grouped[:].rearrange("p m j -> p (m j)"))
+            return [(codes[:, m : m + P], plane[:, m : m + P]) for m in range(0, width, P)]
+
+        def product(q, b, quantised, bank_nos):
+            codes, plane = quantised
             rows = sb("rows%d%d" % (q, b), [P, S], F32)
             width = S // len(bank_nos)
             for h, bank_no in enumerate(bank_nos):
                 cols = slice(h * width, (h + 1) * width)
                 acc = bank(bank_no, [P, width])
                 nc.tensor.matmul_mx(
-                    acc[:], lhsT=codes[:].bitcast(FP8X4), lhsT_scale=plane[:],
+                    acc[:], lhsT=codes.bitcast(FP8X4), lhsT_scale=plane,
                     rhs=picked_words[:, cols].bitcast(FP8X4), rhs_scale=picked_scales[:, cols], start=True, stop=True,
                 )
                 nc.scalar.copy(rows[:, cols], acc[:])
@@ -100,27 +106,27 @@ def tile_picked_yskinlb_norm_p_kernel(
             for c in range(CHUNKS):
                 nc.tensor.matmul(dst[:, c, :], src[:, c, :], ident[:], start=(first and c == 0), stop=(last and c == CHUNKS - 1), is_transpose=True)
 
-        def turn_rest(name, src, sign, bank_no):
+        def turn_rest(turned, src, sign, bank_no):
             both = bank(bank_no, [P, BLOCKS, CHUNKS, P])
             for b in range(BLOCKS):
                 turn(both[:, b], src[:, b, :].rearrange("p (c r) -> p c r", c=CHUNKS), b == 0, b == BLOCKS - 1)
-            turned = sb(name, [P, BLOCKS, CHUNKS, P], F32)
-            nc.scalar.activation(turned[:], both[:], ACT.Copy, scale=sign)
-            return turned
+            nc.scalar.activation(turned, both[:], ACT.Copy, scale=sign)
 
-        def mix(q, b, rows, bank_no):
+        def term(name, tag=None):
+            return sb(name, [P, CHUNKS, P], F32, tag=tag)[:]
+
+        def mix(q, b, rows, bank_no, terms):
             mixed = bank(bank_no, [P, CHUNKS, P])
             for d in range(2):
-                term = sb("term%d%d%d" % (q, b, d), [P, CHUNKS, P], F32)
-                fetch(term[:], rows, d)
-                turn(mixed, term, d == 0, d == 1)
+                fetch(terms[d], rows, d)
+                turn(mixed, terms[d], d == 0, d == 1)
             return mixed
 
         def spread(q, b, mixed, rest_t, sumsq, numer):
-            square = sb("square%d%d" % (q, b), [P, CHUNKS, P], F32)
-            nc.scalar.activation(square[:], mixed[:], ACT.Square)
+            square = squares[:, q, b]
             moved = sb("moved%d%d" % (q, b), [P, CHUNKS, P], F32)
             nc.vector.tensor_tensor(moved[:], mixed[:], rest_t[:, b], MULT)
+            nc.scalar.activation(square, mixed[:], ACT.Square)
             turn(sumsq, square, q == 0, q == 1)
             turn(numer, moved, q == 0, q == 1)
 
@@ -138,24 +144,50 @@ def tile_picked_yskinlb_norm_p_kernel(
             nc.vector.tensor_tensor(result[:], half[:], terms[1], ADD)
             nc.sync.dma_start(out[b * P : (b + 1) * P, :], result[:].rearrange("p c r -> p (c r)"))
 
-        ra = [product(0, 0, nc.scalar.copy, [6, 0]), product(0, 1, nc.vector.tensor_copy, [1])]
-        rb = [product(1, 0, nc.vector.tensor_copy, [2]), product(1, 1, nc.scalar.copy, [3])]
-        tr = [product(2, b, nc.scalar.copy, [b]) for b in range(BLOCKS)]
-        aa = [mix(0, b, ra[b], 2 + b) for b in range(BLOCKS)]
-        px_t = turn_rest("px_t", px_sb, 1.0, 4)
-        py_t = turn_rest("py_t", py_sb, -1.0, 5)
-        sumsq = [bank(4, [P, CHUNKS, P]), bank(6, [P, CHUNKS, P])]
-        numer = [bank(5, [P, CHUNKS, P]), bank(7, [P, CHUNKS, P])]
-        bb0 = mix(1, 0, rb[0], 0)
+        def finish_turned(b, rotated, terms):
+            total_t = bank(5, [P, CHUNKS, P])
+            turn(total_t, terms[1], True, False)
+            turn(total_t, terms[0], False, False)
+            turn(total_t, rotated, False, True)
+            total_sb = sb("total_sb", [P, CHUNKS, P], F32)
+            nc.scalar.copy(total_sb[:], total_t[:])
+            total = bank(2, [P, CHUNKS, P])
+            turn(total, total_sb, True, True)
+            result = sb("result%d" % b, [P, CHUNKS, P], F32)
+            nc.scalar.copy(result[:], total[:])
+            nc.sync.dma_start(out[b * P : (b + 1) * P, :], result[:].rearrange("p c r -> p (c r)"))
+
+        ra = [
+            product(0, 0, quantise("w1a", w1_raw[:, :, 0:P], nc.vector.tensor_copy, "stage0")[0], [0, 1]),
+            product(0, 1, quantise("w1b", w1_raw[:, :, P : 2 * P], nc.scalar.copy, "stage1")[0], [2]),
+        ]
+        w2_q = quantise("w2", w2_raw[:], nc.vector.tensor_copy, "stage1")
+        rb = [product(1, b, w2_q[b], [3 + b]) for b in range(BLOCKS)]
+        aa0 = mix(0, 0, ra[0], 5, [term("a00"), term("a01", "stage1")])
+        w3_q = quantise("w3", w3_raw[:], nc.scalar.copy, "rows00")
+        rest_t = sb("rest_t", [P, 2, BLOCKS, CHUNKS, P], F32, tag="w3_raw")
+        px_t, py_t = rest_t[:, 0], rest_t[:, 1]
+        turn_rest(px_t, px_sb, 1.0, 3)
+        turn_rest(py_t, py_sb, -1.0, 4)
+        tr = [product(2, b, w3_q[b], [b]) for b in range(BLOCKS)]
+        squares = sb("squares", [P, 2, BLOCKS, CHUNKS, P], F32)
+        aa = [
+            aa0,
+            mix(0, 1, ra[1], 2, [term("a10"), term("a11")]),
+        ]
+        bb0 = mix(1, 0, rb[0], 0, [term("b00"), term("b01", "rows00")])
+        sumsq, numer = [], []
         for b in range(BLOCKS):
+            sumsq.append(bank((3, 6)[b], [P, CHUNKS, P]))
+            numer.append(bank((4, 7)[b], [P, CHUNKS, P]))
             spread(0, b, aa[b], px_t, sumsq[b], numer[b])
-        bb = [bb0, mix(1, 1, rb[1], 1)]
-        shifts = []
+        bb = [bb0, mix(1, 1, rb[1], 1, [term("b10"), px_t[:, 1]])]
+        shift01 = term("t01")
+        fetch(shift01, tr[0], 1)
         for b in range(BLOCKS):
             spread(1, b, bb[b], py_t, sumsq[b], numer[b])
-            second = sb("shift%d" % b, [P, CHUNKS, P], F32)
             fetch(py_t[:, b], tr[b], 0)
-            fetch(second[:], tr[b], 1)
-            shifts.append([py_t[:, b], second[:]])
-        for b in range(BLOCKS):
-            finish(b, normalise(b, sumsq[b], numer[b]), shifts[b])
+        finish_turned(0, normalise(0, sumsq[0], numer[0]), [py_t[:, 0], shift01])
+        shift11 = term("t11", "inv0")
+        fetch(shift11, tr[1], 1)
+        finish(1, normalise(1, sumsq[1], numer[1]), [py_t[:, 1], shift11])

@@ -19,6 +19,9 @@ ADD = mybir.AluOpType.add
 
 P = 128
 PACK = 4
+GROUP = 16
+QUADRANT = 32
+RUN = 4
 BLOCKS = N // P
 CHUNKS = U // P
 EPS = 0.1
@@ -35,11 +38,14 @@ def tile_picked_yskinlb_norm_p_kernel(
         def bank(i, shape):
             return psum.tile(shape, F32, name="bank%d" % i)
 
-        def sb(name, shape, dtype, tag=None):
-            return keep.tile(shape, dtype, name=name, tag=tag or name, align_bytes=64)
+        def sb(name, shape, dtype, over=None):
+            return keep.tile(shape, dtype, name=name, tag=over or name, align_bytes=64)
 
-        offs_sb = keep.tile([P, S // 16], U16, name="offs_sb")
-        jt_sb = [keep.tile([P, U // 16], U16, name="jt%d_sb" % d) for d in range(2)]
+        def block_tile(name, over=None):
+            return sb(name, [P, CHUNKS, P], F32, over)[:]
+
+        offs_sb = keep.tile([P, S // GROUP], U16, name="offs_sb")
+        jt_sb = [keep.tile([P, U // GROUP], U16, name="jt%d_sb" % d) for d in range(2)]
         words = sb("words", [P, T], I32)
         scales = sb("scales", [P, T], U8)
         w1_raw = sb("w1_raw", [P, PACK, N], F32)
@@ -59,15 +65,16 @@ def tile_picked_yskinlb_norm_p_kernel(
         nc.sync.dma_start(offs_sb[:], offs)
         nc.sync.dma_start(jt_sb[0][:], jt1)
         nc.sync.dma_start(jt_sb[1][:], jt2)
-        for q in range(4):
-            nc.sync.dma_start(scales[32 * q : 32 * q + 4, :].bitcast(I32), x_scales[0, 4 * q : 4 * q + 4, :].bitcast(I32))
+        for q in range(P // QUADRANT):
+            rows_of_quadrant = x_scales[0, PACK * q : PACK * (q + 1), :]
+            nc.sync.dma_start(scales[QUADRANT * q : QUADRANT * q + PACK, :].bitcast(I32), rows_of_quadrant.bitcast(I32))
         nc.sync.dma_start(words[:], x_words[0].rearrange("p n t -> p (n t)").bitcast(I32))
         nc.sync.dma_start(w1_raw[:], w1.rearrange("(p j) m -> p j m", j=PACK))
         nc.sync.dma_start(w2_raw[:], w2.rearrange("(p j) m -> p j m", j=PACK))
         nc.sync.dma_start(wgt_sb[:], wgt.rearrange("d p r -> p d r"))
-        nc.sync.dma_start(w3_raw[:], w3.rearrange("(p j) m -> p j m", j=PACK))
         nc.sync.dma_start(px_sb[:], px.rearrange("(b p) r -> p b r", p=P))
         nc.sync.dma_start(py_sb[:], py.rearrange("(b p) r -> p b r", p=P))
+        nc.sync.dma_start(w3_raw[:], w3.rearrange("(p j) m -> p j m", j=PACK))
 
         nc.scalar.activation(warm[:], one[:], ACT.Abs_reciprocal_sqrt)
 
@@ -78,23 +85,28 @@ def tile_picked_yskinlb_norm_p_kernel(
 
         def quantise(name, raw, cast, stage):
             width = raw.shape[2]
-            grouped = sb(name + "_grouped", [P, width, PACK], BF16, tag=stage)
-            cast(grouped[:].rearrange("p (c i) j -> p c j i", i=4), raw.rearrange("p j (c i) -> p c j i", i=4))
+            grouped = sb(name + "_grouped", [P, width, PACK], BF16, stage)
+            cast(grouped[:].rearrange("p (c i) j -> p c j i", i=RUN), raw.rearrange("p j (c i) -> p c j i", i=RUN))
             codes = sb(name + "_codes", [P, width], U32)
-            plane = sb(name + "_plane", [P, width], U8)
-            nc.vector.quantize_mx(codes[:].bitcast(FP8X4), plane[:], grouped[:].rearrange("p m j -> p (m j)"))
-            return [(codes[:, m : m + P], plane[:, m : m + P]) for m in range(0, width, P)]
+            scale_bytes = sb(name + "_scale_bytes", [P, width], U8)
+            nc.vector.quantize_mx(codes[:].bitcast(FP8X4), scale_bytes[:], grouped[:].rearrange("p m j -> p (m j)"))
+            return [(codes[:, m : m + P], scale_bytes[:, m : m + P]) for m in range(0, width, P)]
 
-        def product(q, b, quantised, bank_nos):
-            codes, plane = quantised
-            rows = sb("rows%d%d" % (q, b), [P, S], F32)
-            width = S // len(bank_nos)
-            for h, bank_no in enumerate(bank_nos):
+        def product(name, quantised, banks):
+            codes, scale_bytes = quantised
+            rows = sb(name, [P, S], F32)
+            width = S // len(banks)
+            for h, bank_no in enumerate(banks):
                 cols = slice(h * width, (h + 1) * width)
                 acc = bank(bank_no, [P, width])
                 nc.tensor.matmul_mx(
-                    acc[:], lhsT=codes.bitcast(FP8X4), lhsT_scale=plane,
-                    rhs=picked_words[:, cols].bitcast(FP8X4), rhs_scale=picked_scales[:, cols], start=True, stop=True,
+                    acc[:],
+                    lhsT=codes.bitcast(FP8X4),
+                    lhsT_scale=scale_bytes,
+                    rhs=picked_words[:, cols].bitcast(FP8X4),
+                    rhs_scale=picked_scales[:, cols],
+                    start=True,
+                    stop=True,
                 )
                 nc.scalar.copy(rows[:, cols], acc[:])
             return rows
@@ -104,90 +116,96 @@ def tile_picked_yskinlb_norm_p_kernel(
 
         def turn(dst, src, first, last):
             for c in range(CHUNKS):
-                nc.tensor.matmul(dst[:, c, :], src[:, c, :], ident[:], start=(first and c == 0), stop=(last and c == CHUNKS - 1), is_transpose=True)
+                opens, closes = first and c == 0, last and c == CHUNKS - 1
+                nc.tensor.matmul(dst[:, c, :], src[:, c, :], ident[:], start=opens, stop=closes, is_transpose=True)
 
-        def turn_rest(turned, src, sign, bank_no):
+        def turn_rest(turned, rest, sign, bank_no):
             both = bank(bank_no, [P, BLOCKS, CHUNKS, P])
             for b in range(BLOCKS):
-                turn(both[:, b], src[:, b, :].rearrange("p (c r) -> p c r", c=CHUNKS), b == 0, b == BLOCKS - 1)
+                turn(both[:, b], rest[:, b, :].rearrange("p (c r) -> p c r", c=CHUNKS), b == 0, b == BLOCKS - 1)
             nc.scalar.activation(turned, both[:], ACT.Copy, scale=sign)
 
-        def term(name, tag=None):
-            return sb(name, [P, CHUNKS, P], F32, tag=tag)[:]
-
-        def mix(q, b, rows, bank_no, terms):
+        def mix(rows, bank_no, terms):
             mixed = bank(bank_no, [P, CHUNKS, P])
             for d in range(2):
                 fetch(terms[d], rows, d)
                 turn(mixed, terms[d], d == 0, d == 1)
             return mixed
 
-        def spread(q, b, mixed, rest_t, sumsq, numer):
-            square = squares[:, q, b]
-            moved = sb("moved%d%d" % (q, b), [P, CHUNKS, P], F32)
-            nc.vector.tensor_tensor(moved[:], mixed[:], rest_t[:, b], MULT)
-            nc.scalar.activation(square, mixed[:], ACT.Square)
-            turn(sumsq, square, q == 0, q == 1)
-            turn(numer, moved, q == 0, q == 1)
+        def open_sums(b, aa, bank_sumsq, bank_numer):
+            sumsq = bank(bank_sumsq, [P, CHUNKS, P])
+            numer = bank(bank_numer, [P, CHUNKS, P])
+            moved = block_tile("aa_px%d" % b)
+            nc.vector.tensor_tensor(moved, aa[:], px_t[:, b], MULT)
+            nc.scalar.activation(squares[:, 0, b], aa[:], ACT.Square)
+            turn(sumsq, squares[:, 0, b], True, False)
+            turn(numer, moved, True, False)
+            return sumsq, numer
+
+        def close_sums(b, bb, sumsq, numer):
+            moved = block_tile("bb_py%d" % b)
+            nc.scalar.activation(squares[:, 1, b], bb[:], ACT.Square)
+            nc.vector.tensor_tensor(moved, bb[:], py_t[:, b], MULT)
+            turn(sumsq, squares[:, 1, b], False, True)
+            turn(numer, moved, False, True)
 
         def normalise(b, sumsq, numer):
-            inv = sb("inv%d" % b, [P, CHUNKS, P], F32)
-            nc.scalar.activation(inv[:], sumsq[:], ACT.Abs_reciprocal_sqrt, bias=EPS)
-            rotated = sb("rotated%d" % b, [P, CHUNKS, P], F32)
-            nc.vector.tensor_tensor(rotated[:], numer[:], inv[:], MULT)
+            inv = block_tile("inv%d" % b)
+            nc.scalar.activation(inv, sumsq[:], ACT.Abs_reciprocal_sqrt, bias=EPS)
+            rotated = block_tile("rotated%d" % b)
+            nc.vector.tensor_tensor(rotated, numer[:], inv, MULT)
             return rotated
 
-        def finish(b, rotated, terms):
-            half = sb("half%d" % b, [P, CHUNKS, P], F32)
-            nc.vector.tensor_tensor(half[:], rotated[:], terms[0], ADD)
-            result = sb("result%d" % b, [P, CHUNKS, P], F32)
-            nc.vector.tensor_tensor(result[:], half[:], terms[1], ADD)
-            nc.sync.dma_start(out[b * P : (b + 1) * P, :], result[:].rearrange("p c r -> p (c r)"))
+        def store(b, result):
+            nc.sync.dma_start(out[b * P : (b + 1) * P, :], result.rearrange("p c r -> p (c r)"))
 
-        def finish_turned(b, rotated, terms):
-            total_t = bank(5, [P, CHUNKS, P])
-            turn(total_t, terms[1], True, False)
-            turn(total_t, terms[0], False, False)
-            turn(total_t, rotated, False, True)
-            total_sb = sb("total_sb", [P, CHUNKS, P], F32)
-            nc.scalar.copy(total_sb[:], total_t[:])
-            total = bank(2, [P, CHUNKS, P])
-            turn(total, total_sb, True, True)
-            result = sb("result%d" % b, [P, CHUNKS, P], F32)
-            nc.scalar.copy(result[:], total[:])
-            nc.sync.dma_start(out[b * P : (b + 1) * P, :], result[:].rearrange("p c r -> p (c r)"))
+        ra0 = product("ra0", quantise("w1a", w1_raw[:, :, 0:P], nc.vector.tensor_copy, "stage_a")[0], [0, 1])
+        ra1 = product("ra1", quantise("w1b", w1_raw[:, :, P:N], nc.scalar.copy, "stage_b")[0], [2])
+        w2_q = quantise("w2", w2_raw[:], nc.vector.tensor_copy, "stage_b")
+        rb = [product("rb%d" % b, w2_q[b], [3 + b]) for b in range(BLOCKS)]
 
-        ra = [
-            product(0, 0, quantise("w1a", w1_raw[:, :, 0:P], nc.vector.tensor_copy, "stage0")[0], [0, 1]),
-            product(0, 1, quantise("w1b", w1_raw[:, :, P : 2 * P], nc.scalar.copy, "stage1")[0], [2]),
-        ]
-        w2_q = quantise("w2", w2_raw[:], nc.vector.tensor_copy, "stage1")
-        rb = [product(1, b, w2_q[b], [3 + b]) for b in range(BLOCKS)]
-        aa0 = mix(0, 0, ra[0], 5, [term("a00"), term("a01", "stage1")])
-        w3_q = quantise("w3", w3_raw[:], nc.scalar.copy, "rows00")
-        rest_t = sb("rest_t", [P, 2, BLOCKS, CHUNKS, P], F32, tag="w3_raw")
+        rest_t = sb("rest_t", [P, 2, BLOCKS, CHUNKS, P], F32)
         px_t, py_t = rest_t[:, 0], rest_t[:, 1]
-        turn_rest(px_t, px_sb, 1.0, 3)
-        turn_rest(py_t, py_sb, -1.0, 4)
-        tr = [product(2, b, w3_q[b], [b]) for b in range(BLOCKS)]
+        turn_rest(px_t, px_sb, 1.0, 0)
+        turn_rest(py_t, py_sb, -1.0, 1)
+
+        aa0 = mix(ra0, 5, [block_tile("aa0_term0"), block_tile("aa0_term1")])
+        w3_q = quantise("w3", w3_raw[:], nc.scalar.copy, "py_sb")
+        tr = [product("tr%d" % b, w3_q[b], [6 + b]) for b in range(BLOCKS)]
         squares = sb("squares", [P, 2, BLOCKS, CHUNKS, P], F32)
-        aa = [
-            aa0,
-            mix(0, 1, ra[1], 2, [term("a10"), term("a11")]),
-        ]
-        bb0 = mix(1, 0, rb[0], 0, [term("b00"), term("b01", "rows00")])
-        sumsq, numer = [], []
-        for b in range(BLOCKS):
-            sumsq.append(bank((3, 6)[b], [P, CHUNKS, P]))
-            numer.append(bank((4, 7)[b], [P, CHUNKS, P]))
-            spread(0, b, aa[b], px_t, sumsq[b], numer[b])
-        bb = [bb0, mix(1, 1, rb[1], 1, [term("b10"), px_t[:, 1]])]
-        shift01 = term("t01")
-        fetch(shift01, tr[0], 1)
-        for b in range(BLOCKS):
-            spread(1, b, bb[b], py_t, sumsq[b], numer[b])
-            fetch(py_t[:, b], tr[b], 0)
-        finish_turned(0, normalise(0, sumsq[0], numer[0]), [py_t[:, 0], shift01])
-        shift11 = term("t11", "inv0")
-        fetch(shift11, tr[1], 1)
-        finish(1, normalise(1, sumsq[1], numer[1]), [py_t[:, 1], shift11])
+        aa1 = mix(ra1, 2, [block_tile("aa1_term0"), block_tile("aa1_term1")])
+        sums0 = open_sums(0, aa0, 3, 4)
+        sums1 = open_sums(1, aa1, 6, 7)
+
+        bb0 = mix(rb[0], 0, [block_tile("bb0_term0"), px_t[:, 0]])
+        bb1_terms = sb("bb1_terms", [P, 2, CHUNKS, P], F32, "py_sb")
+        bb1 = mix(rb[1], 1, [bb1_terms[:, 0], bb1_terms[:, 1]])
+
+        close_sums(0, bb0, *sums0)
+        tt0_term0, tt0_term1 = py_t[:, 0], px_t[:, 1]
+        fetch(tt0_term1, tr[0], 1)
+        fetch(tt0_term0, tr[0], 0)
+        rotated0 = normalise(0, *sums0)
+        total_t = bank(5, [P, CHUNKS, P])
+        turn(total_t, tt0_term1, True, False)
+        turn(total_t, tt0_term0, False, False)
+        turn(total_t, rotated0, False, True)
+        total_t_sb = block_tile("total_t_sb")
+        nc.scalar.copy(total_t_sb, total_t[:])
+        total = bank(2, [P, CHUNKS, P])
+        turn(total, total_t_sb, True, True)
+        result0 = block_tile("result0")
+        nc.scalar.copy(result0, total[:])
+        store(0, result0)
+
+        close_sums(1, bb1, *sums1)
+        tt1_term0 = py_t[:, 1]
+        fetch(tt1_term0, tr[1], 0)
+        tt1_term1 = block_tile("tt1_term1", "inv0")
+        fetch(tt1_term1, tr[1], 1)
+        rotated1 = normalise(1, *sums1)
+        tt1 = block_tile("tt1")
+        nc.vector.tensor_tensor(tt1, tt1_term0, tt1_term1, ADD)
+        result1 = block_tile("result1")
+        nc.vector.tensor_tensor(result1, tt1, rotated1, ADD)
+        store(1, result1)

from contextlib import ExitStack

import concourse.mybir as mybir
from concourse.masks import make_identity

K, T, S, N, U = 512, 1024, 512, 256, 256
FLOPS = 3 * 2 * K * N * S

F32 = mybir.dt.float32
BF16 = mybir.dt.bfloat16
I32 = mybir.dt.int32
U32 = mybir.dt.uint32
U16 = mybir.dt.uint16
U8 = mybir.dt.uint8
FP8X4 = mybir.dt.float8_e4m3fn_x4
ACT = mybir.ActivationFunctionType
MULT = mybir.AluOpType.mult
ADD = mybir.AluOpType.add

P = 128
PACK = 4
GROUP = 16
QUADRANT = 32
RUN = 4
BLOCKS = N // P
CHUNKS = U // P
EPS = 0.1


def tile_picked_yskinlb_norm_p_kernel(
    tc, x_words, x_scales, w1, w2, w3, px, py, wgt, offs, jt1, jt2, out
):
    nc = tc.nc
    with ExitStack() as ctx:
        keep = ctx.enter_context(tc.tile_pool(name="keep", bufs=1))
        psum = ctx.enter_context(tc.psum_pool(name="psum", bufs=1))

        def bank(i, shape):
            return psum.tile(shape, F32, name="bank%d" % i)

        def sb(name, shape, dtype, over=None):
            return keep.tile(shape, dtype, name=name, tag=over or name, align_bytes=64)

        def block_tile(name, over=None):
            return sb(name, [P, CHUNKS, P], F32, over)[:]

        offs_sb = keep.tile([P, S // GROUP], U16, name="offs_sb")
        jt_sb = [keep.tile([P, U // GROUP], U16, name="jt%d_sb" % d) for d in range(2)]
        words = sb("words", [P, T], I32)
        scales = sb("scales", [P, T], U8)
        w1_raw = sb("w1_raw", [P, PACK, N], F32)
        w2_raw = sb("w2_raw", [P, PACK, N], F32)
        w3_raw = sb("w3_raw", [P, PACK, N], F32)
        wgt_sb = sb("wgt_sb", [P, 2, U], F32)
        px_sb = sb("px_sb", [P, BLOCKS, U], F32)
        py_sb = sb("py_sb", [P, BLOCKS, U], F32)
        ident = sb("ident", [P, P], F32)
        one = sb("one", [P, 1], F32)
        warm = sb("warm", [P, 1], F32)

        nc.gpsimd.memset(scales[:].bitcast(I32), 0)
        nc.gpsimd.memset(one[:], 1.0)
        make_identity(nc, ident[:])

        nc.sync.dma_start(offs_sb[:], offs)
        nc.sync.dma_start(jt_sb[0][:], jt1)
        nc.sync.dma_start(jt_sb[1][:], jt2)
        for q in range(P // QUADRANT):
            rows_of_quadrant = x_scales[0, PACK * q : PACK * (q + 1), :]
            nc.sync.dma_start(scales[QUADRANT * q : QUADRANT * q + PACK, :].bitcast(I32), rows_of_quadrant.bitcast(I32))
        nc.sync.dma_start(words[:], x_words[0].rearrange("p n t -> p (n t)").bitcast(I32))
        nc.sync.dma_start(w1_raw[:], w1.rearrange("(p j) m -> p j m", j=PACK))
        nc.sync.dma_start(w2_raw[:], w2.rearrange("(p j) m -> p j m", j=PACK))
        nc.sync.dma_start(wgt_sb[:], wgt.rearrange("d p r -> p d r"))
        nc.sync.dma_start(px_sb[:], px.rearrange("(b p) r -> p b r", p=P))
        nc.sync.dma_start(py_sb[:], py.rearrange("(b p) r -> p b r", p=P))
        nc.sync.dma_start(w3_raw[:], w3.rearrange("(p j) m -> p j m", j=PACK))

        nc.scalar.activation(warm[:], one[:], ACT.Abs_reciprocal_sqrt)

        picked_scales = sb("picked_scales", [P, S], U8)
        nc.vector.tensor_copy(picked_scales[:], scales[:].indirect(offs_sb[:]))
        picked_words = sb("picked_words", [P, S], U32)
        nc.vector.tensor_copy(picked_words[:], words[:].bitcast(U32).indirect(offs_sb[:]))

        def quantise(name, raw, cast, stage):
            width = raw.shape[2]
            grouped = sb(name + "_grouped", [P, width, PACK], BF16, stage)
            cast(grouped[:].rearrange("p (c i) j -> p c j i", i=RUN), raw.rearrange("p j (c i) -> p c j i", i=RUN))
            codes = sb(name + "_codes", [P, width], U32)
            scale_bytes = sb(name + "_scale_bytes", [P, width], U8)
            nc.vector.quantize_mx(codes[:].bitcast(FP8X4), scale_bytes[:], grouped[:].rearrange("p m j -> p (m j)"))
            return [(codes[:, m : m + P], scale_bytes[:, m : m + P]) for m in range(0, width, P)]

        def product(name, quantised, banks):
            codes, scale_bytes = quantised
            rows = sb(name, [P, S], F32)
            width = S // len(banks)
            for h, bank_no in enumerate(banks):
                cols = slice(h * width, (h + 1) * width)
                acc = bank(bank_no, [P, width])
                nc.tensor.matmul_mx(
                    acc[:],
                    lhsT=codes.bitcast(FP8X4),
                    lhsT_scale=scale_bytes,
                    rhs=picked_words[:, cols].bitcast(FP8X4),
                    rhs_scale=picked_scales[:, cols],
                    start=True,
                    stop=True,
                )
                nc.scalar.copy(rows[:, cols], acc[:])
            return rows

        def fetch(dst, rows, d):
            nc.vector.tensor_tensor(dst.rearrange("p c r -> p (c r)"), rows[:].indirect(jt_sb[d][:]), wgt_sb[:, d, :], MULT)

        def turn(dst, src, first, last):
            for c in range(CHUNKS):
                opens, closes = first and c == 0, last and c == CHUNKS - 1
                nc.tensor.matmul(dst[:, c, :], src[:, c, :], ident[:], start=opens, stop=closes, is_transpose=True)

        def turn_rest(turned, rest, sign, bank_no):
            both = bank(bank_no, [P, BLOCKS, CHUNKS, P])
            for b in range(BLOCKS):
                turn(both[:, b], rest[:, b, :].rearrange("p (c r) -> p c r", c=CHUNKS), b == 0, b == BLOCKS - 1)
            nc.scalar.activation(turned, both[:], ACT.Copy, scale=sign)

        def mix(rows, bank_no, terms):
            mixed = bank(bank_no, [P, CHUNKS, P])
            for d in range(2):
                fetch(terms[d], rows, d)
                turn(mixed, terms[d], d == 0, d == 1)
            return mixed

        def open_sums(b, aa, bank_sumsq, bank_numer):
            sumsq = bank(bank_sumsq, [P, CHUNKS, P])
            numer = bank(bank_numer, [P, CHUNKS, P])
            moved = block_tile("aa_px%d" % b)
            nc.vector.tensor_tensor(moved, aa[:], px_t[:, b], MULT)
            nc.scalar.activation(squares[:, 0, b], aa[:], ACT.Square)
            turn(sumsq, squares[:, 0, b], True, False)
            turn(numer, moved, True, False)
            return sumsq, numer

        def close_sums(b, bb, sumsq, numer):
            moved = block_tile("bb_py%d" % b)
            nc.scalar.activation(squares[:, 1, b], bb[:], ACT.Square)
            nc.vector.tensor_tensor(moved, bb[:], py_t[:, b], MULT)
            turn(sumsq, squares[:, 1, b], False, True)
            turn(numer, moved, False, True)

        def normalise(b, sumsq, numer):
            inv = block_tile("inv%d" % b)
            nc.scalar.activation(inv, sumsq[:], ACT.Abs_reciprocal_sqrt, bias=EPS)
            rotated = block_tile("rotated%d" % b)
            nc.vector.tensor_tensor(rotated, numer[:], inv, MULT)
            return rotated

        def store(b, result):
            nc.sync.dma_start(out[b * P : (b + 1) * P, :], result.rearrange("p c r -> p (c r)"))

        ra0 = product("ra0", quantise("w1a", w1_raw[:, :, 0:P], nc.vector.tensor_copy, "stage_a")[0], [0, 1])
        ra1 = product("ra1", quantise("w1b", w1_raw[:, :, P:N], nc.scalar.copy, "stage_b")[0], [2])
        w2_q = quantise("w2", w2_raw[:], nc.vector.tensor_copy, "stage_b")
        rb = [product("rb%d" % b, w2_q[b], [3 + b]) for b in range(BLOCKS)]

        rest_t = sb("rest_t", [P, 2, BLOCKS, CHUNKS, P], F32)
        px_t, py_t = rest_t[:, 0], rest_t[:, 1]
        turn_rest(px_t, px_sb, 1.0, 0)
        turn_rest(py_t, py_sb, -1.0, 1)

        aa0 = mix(ra0, 5, [block_tile("aa0_term0"), block_tile("aa0_term1")])
        w3_q = quantise("w3", w3_raw[:], nc.scalar.copy, "py_sb")
        tr = [product("tr%d" % b, w3_q[b], [6 + b]) for b in range(BLOCKS)]
        squares = sb("squares", [P, 2, BLOCKS, CHUNKS, P], F32)
        aa1 = mix(ra1, 2, [block_tile("aa1_term0"), block_tile("aa1_term1")])
        sums0 = open_sums(0, aa0, 3, 4)
        sums1 = open_sums(1, aa1, 6, 7)

        bb0 = mix(rb[0], 0, [block_tile("bb0_term0"), px_t[:, 0]])
        bb1_terms = sb("bb1_terms", [P, 2, CHUNKS, P], F32, "py_sb")
        bb1 = mix(rb[1], 1, [bb1_terms[:, 0], bb1_terms[:, 1]])

        close_sums(0, bb0, *sums0)
        tt0_term0, tt0_term1 = py_t[:, 0], px_t[:, 1]
        fetch(tt0_term1, tr[0], 1)
        fetch(tt0_term0, tr[0], 0)
        rotated0 = normalise(0, *sums0)
        total_t = bank(5, [P, CHUNKS, P])
        turn(total_t, tt0_term1, True, False)
        turn(total_t, tt0_term0, False, False)
        turn(total_t, rotated0, False, True)
        total_t_sb = block_tile("total_t_sb")
        nc.scalar.copy(total_t_sb, total_t[:])
        total = bank(2, [P, CHUNKS, P])
        turn(total, total_t_sb, True, True)
        result0 = block_tile("result0")
        nc.scalar.copy(result0, total[:])
        store(0, result0)

        close_sums(1, bb1, *sums1)
        tt1_term0 = py_t[:, 1]
        fetch(tt1_term0, tr[1], 0)
        tt1_term1 = block_tile("tt1_term1", "inv0")
        fetch(tt1_term1, tr[1], 1)
        rotated1 = normalise(1, *sums1)
        tt1 = block_tile("tt1")
        nc.vector.tensor_tensor(tt1, tt1_term0, tt1_term1, ADD)
        result1 = block_tile("result1")
        nc.vector.tensor_tensor(result1, tt1, rotated1, ADD)
        store(1, result1)
